import numpy as np
import ml_dtypes


def mxq(x, axis, fmt="e4m3"):
    dtype, down = {"e4m3": (ml_dtypes.float8_e4m3fn, 7), "e5m2": (ml_dtypes.float8_e5m2, 14)}[fmt]
    v = np.moveaxis(np.asarray(x, np.float32).astype(ml_dtypes.bfloat16).astype(np.float64), axis, -1)
    blocks = v.reshape(v.shape[:-1] + (-1, 32))
    amax = np.abs(blocks).max(-1, keepdims=True)
    byte = np.maximum(np.where(amax > 0, np.frexp(amax)[1] - 1 + 127, 0) - down, 1)
    scale = np.exp2(byte - 127.0)
    codes = (blocks / scale).astype(np.float32).astype(dtype).astype(np.float64)
    return np.moveaxis((codes * scale).reshape(v.shape), -1, axis)


WIDE = False


def mx_kscale(k):
    if not WIDE:
        return np.ones(k)
    levels = np.array([10, -10, 5, -5, 0])
    if k % 512:
        return np.exp2(np.random.permutation(np.resize(levels, k // 32))).repeat(32)
    a = np.empty((k // 512, 16))
    for p in range(k // 512):
        a[p, :8] = np.random.permutation(np.resize(levels, 8))
        for g in range(8):
            far = levels[np.abs(levels - a[p, g]) >= 10]
            a[p, g + 8] = far[np.random.randint(len(far))]
    return np.exp2(a.ravel()).repeat(32)


def f64(x):
    return np.asarray(x).astype(np.float64)


def striped(idx):
    return np.tile(np.asarray(idx).reshape(-1, 16).T, (8, 1)).astype(np.uint16)


def unstriped(offs):
    return offs[:16].T.reshape(-1).astype(np.int64)


def striped8(idx):
    return np.asarray(idx).reshape(8, -1, 16).transpose(0, 2, 1).reshape(128, -1).astype(np.uint16)


def unstriped8(offs):
    return offs.reshape(8, 16, -1).transpose(0, 2, 1).reshape(8, -1).astype(np.int64)


def pick8(x, idx, run):
    r = np.arange(len(x))
    return x[r[:, None], idx[r % (8 * run) // run]]


E2M1 = np.array([0.0, 0.5, 1.0, 1.5, 2.0, 3.0, 4.0, 6.0, -0.0, -0.5, -1.0, -1.5, -2.0, -3.0, -4.0, -6.0])


def pack_weight(w, fmt):
    k, n = w.shape
    w = f64(np.asarray(w, np.float32).astype(ml_dtypes.bfloat16)).reshape(k // 32, 32, n)
    amax = np.abs(w).max(1)
    if fmt == "e4m3":
        byte = np.frexp(amax)[1] - 1 + 127 - 7
    else:
        mant, ex = np.frexp(amax / 6.0)
        byte = np.where(mant > 0.5, ex, ex - 1) + 127
    byte = np.clip(np.where(amax > 0, byte, 1), 1, 254)
    scaled = (w * np.exp2(127.0 - byte)[:, None, :]).reshape(k, n).astype(np.float32)
    by_word = np.ascontiguousarray(scaled.reshape(k // 512, 128, 4, n).transpose(0, 1, 3, 2))
    if fmt == "e4m3":
        words = by_word.astype(ml_dtypes.float8_e4m3fn).view(np.uint8)
    else:
        c = by_word.astype(ml_dtypes.float4_e2m1fn).view(np.uint8) & 0xF
        words = (c[..., 0::2] | (c[..., 1::2] << 4)).reshape(k // 512, 128, 2 * n)
    return np.ascontiguousarray(words), np.ascontiguousarray(byte.astype(np.uint8).reshape(k // 512, 16, n))


def unpack_weight(words, scales, fmt):
    g, _, n = scales.shape
    words = np.ascontiguousarray(words).reshape(g, 128, n, -1)
    if fmt == "e4m3":
        vals = words.view(ml_dtypes.float8_e4m3fn).astype(np.float64)
    else:
        nib = np.empty((g, 128, n, 4), np.uint8)
        nib[..., 0::2] = words & 0xF
        nib[..., 1::2] = words >> 4
        vals = E2M1[nib]
    vals = vals * np.repeat(np.exp2(scales.astype(np.float64) - 127.0), 8, axis=1)[..., None]
    return vals.transpose(0, 1, 3, 2).reshape(g * 512, n)


def sgn(shape):
    return np.random.uniform(0.5, 2.0, shape) * np.where(np.random.standard_normal(shape) < 0, -1.0, 1.0)


K, J, R, T, F, G, O, N, U, E = 512, 512, 512, 2048, 2048, 1024, 256, 256, 128, 512


def setup_inputs():
    n = np.random.standard_normal
    idx = np.random.permutation(T)[:J]
    idx2 = np.stack([np.random.permutation(F)[:G] for _ in range(8)])
    idx3 = np.random.permutation(G)[:R]
    idx4 = np.random.permutation(J)[:O]
    idx5 = np.stack([np.random.permutation(J)[:O] for _ in range(8)])
    idx6 = np.stack([np.random.permutation(O)[:U] for _ in range(8)])
    idx7 = np.stack([np.random.permutation(E)[:U] for _ in range(8)])
    fk = mx_kscale(K)
    fr = mx_kscale(R)
    xtp = pack_weight(n((K, T)) * fk[:, None], "e4m3")
    wbp = pack_weight(n((R, N)) * 1 / np.sqrt(R) / fr[:, None], "e4m3")
    return {
        "xt_words": xtp[0],
        "xt_scales": xtp[1],
        "ua": (np.random.randint(-7, 8, (K, F)).astype(np.float64)).astype(np.float32),
        "ha": ((np.random.randint(8, 25, (K, 1)) / 1024.0) / fk[:, None]).astype(np.float32),
        "hb": (np.random.uniform(0.5, 1.6, (K, 1))).astype(np.float32),
        "sa": (np.random.uniform(0.5, 1.6, (R, 1)) * fr[:, None]).astype(np.float32),
        "sb": (np.random.uniform(0.5, 1.6, (R, 1)) * fr[:, None]).astype(np.float32),
        "wb_words": wbp[0],
        "wb_scales": wbp[1],
        "so": (sgn((N, 1))).astype(np.float32),
        "offs": striped(idx),
        "offs2": striped8(idx2),
        "offs3": striped(idx3),
        "offs4": striped(idx4),
        "offs5": striped8(idx5),
        "offs6": striped8(idx6),
        "offs7": striped8(idx7),
    }


def reference(xt_words, xt_scales, ua, ha, hb, sa, sb, wb_words, wb_scales, so, offs, offs2, offs3, offs4, offs5, offs6, offs7):
    idx = unstriped(offs)
    idx2 = unstriped8(offs2)
    idx3 = unstriped(offs3)
    idx4 = unstriped(offs4)
    idx5 = unstriped8(offs5)
    idx6 = unstriped8(offs6)
    idx7 = unstriped8(offs7)
    xtu = unpack_weight(xt_words, xt_scales, "e4m3")
    wbu = unpack_weight(wb_words, wb_scales, "e4m3")
    wcd = pick8(f64(ua), idx2, 64) * f64(ha)
    wc = wcd[:, idx3] * f64(hb)
    wcq = mxq(wc, 0, "e4m3")
    xtidxg = xtu[:, idx]
    a = wcq.T @ xtidxg
    hid = np.maximum(a[:, idx4] * f64(sa), pick8(a, idx5, 64) * f64(sb))
    hidq = mxq(hid, 0, "e4m3")
    p = wbu.T @ hidq
    m0 = pick8(p, idx6, 16) * f64(so)
    y = np.zeros((N, E))
    y[np.arange(N)[:, None], idx7[np.arange(N) % 128 // 16]] = m0
    return y

@@ -1,0 +1,218 @@
+from contextlib import ExitStack
+
+import concourse.mybir as mybir
+
+K, J, R, T, F, G, O, N, U, E = 512, 512, 512, 2048, 2048, 1024, 256, 256, 128, 512
+FLOPS = 2 * K * R * J + 2 * R * N * O
+
+F32 = mybir.dt.float32
+BF16 = mybir.dt.bfloat16
+I32 = mybir.dt.int32
+U32 = mybir.dt.uint32
+U16 = mybir.dt.uint16
+U8 = mybir.dt.uint8
+FP8X4 = mybir.dt.float8_e4m3fn_x4
+COPY = mybir.ActivationFunctionType.Copy
+MAX = mybir.AluOpType.max
+
+P = 128
+PACK = 4
+LANES = 16
+
+
+def tile_picked_tokens_respelled_one_mixedpair_one_posted_kernel(
+    tc, xt_words, xt_scales, ua, ha, hb, sa, sb, wb_words, wb_scales, so,
+    offs, offs2, offs3, offs4, offs5, offs6, offs7, out,
+):
+    nc = tc.nc
+    with ExitStack() as ctx:
+        keep = ctx.enter_context(tc.tile_pool(name="keep", bufs=1))
+        psum = ctx.enter_context(tc.psum_pool(name="psum", bufs=1))
+
+        def load_list(src, name):
+            tile = keep.tile(list(src.shape), U16, name=name)
+            nc.sync.dma_start(tile[:], src)
+            return tile
+
+        def load_rows(queue, src, name):
+            tile = keep.tile([P, PACK], F32, name=name)
+            queue.dma_start(tile[:], src.rearrange("(p j) o -> p (j o)", j=PACK))
+            return tile
+
+        def load_words(src, name):
+            tile = keep.tile([P, src.shape[2]], U32, name=name, align_bytes=64)
+            nc.sync.dma_start(tile[:].bitcast(I32), src[0].rearrange("p n t -> p (n t)").bitcast(I32))
+            return tile
+
+        def load_scales(tile, src):
+            for q in range(4):
+                nc.sync.dma_start(tile[32 * q : 32 * q + 4, :].bitcast(I32), src[0, 4 * q : 4 * q + 4, :].bitcast(I32))
+
+        def entries(lists, first, count):
+            return lists[:, first // LANES : (first + count) // LANES]
+
+        def fetch(dst, window, offsets, scale):
+            nc.scalar.activation(dst, window[:].indirect(offsets), COPY, scale=scale)
+
+        xt_s = keep.tile([P, T], U8, align_bytes=64)
+        wb_s = keep.tile([P, N], U8, align_bytes=64)
+        pages = [keep.tile([P, E], F32, name=f"page{b}") for b in range(N // P)]
+        nc.vector.memset(xt_s[:].bitcast(I32), 0)
+        nc.vector.memset(wb_s[:].bitcast(I32), 0)
+        for page in pages:
+            nc.vector.memset(page[:], 0.0)
+
+        ua_planes = ua.rearrange("(p j) f -> j p f", j=PACK)
+        ua_sb = [keep.tile([P, F], F32, name=f"ua{j}") for j in range(PACK)]
+        ha_sb = load_rows(nc.scalar, ha, "ha_sb")
+        hb_sb = load_rows(nc.scalar, hb, "hb_sb")
+        nc.sync.dma_start(ua_sb[0][:], ua_planes[0])
+        list2 = load_list(offs2, "list2")
+        nc.sync.dma_start(ua_sb[1][:], ua_planes[1])
+        list3 = load_list(offs3, "list3")
+        nc.sync.dma_start(ua_sb[2][:], ua_planes[2])
+        nc.sync.dma_start(ua_sb[3][:], ua_planes[3])
+        list1 = load_list(offs, "list1")
+        xt_w = load_words(xt_words, "xt_w")
+        load_scales(xt_s, xt_scales)
+        list4 = load_list(offs4, "list4")
+        list5 = load_list(offs5, "list5")
+        sa_sb = load_rows(nc.sync, sa, "sa_sb")
+        sb_sb = load_rows(nc.sync, sb, "sb_sb")
+        wb_w = load_words(wb_words, "wb_w")
+        load_scales(wb_s, wb_scales)
+        list6 = load_list(offs6, "list6")
+        list7 = load_list(offs7, "list7")
+        so_sb = keep.tile([P, N // P], F32)
+        with nc.allow_non_contiguous_dma(reason="one weight a partition for each block of output features"):
+            nc.sync.dma_start(so_sb[:], so.rearrange("(b p) o -> p (b o)", p=P))
+
+        wcd = [keep.tile([P, G], F32, name=f"wcd{j}") for j in range(PACK)]
+        wc = keep.tile([P, PACK, R], BF16)
+        wc_in = keep.tile([P, PACK, P, PACK], BF16, align_bytes=64)
+        wc_w = keep.tile([P, R], U32, align_bytes=64)
+        wc_s = keep.tile([P, R], U8, align_bytes=64)
+
+        def spell(j):
+            fetch(wcd[j][:], ua_sb[j], list2[:], ha_sb[:, j : j + 1])
+
+        def read(j, first, count):
+            fetch(wc[:, j, first : first + count], wcd[j], entries(list3, first, count), hb_sb[:, j : j + 1])
+
+        def weave(js, ms, ts):
+            nc.vector.tensor_copy(
+                out=wc_in[:].rearrange("p t m j -> p m t j")[:, ms, ts, js],
+                in_=wc[:].rearrange("p j (m t) -> p m t j", t=PACK)[:, ms, ts, js],
+            )
+
+        spell(0)
+        spell(1)
+        read(0, 0, R)
+        spell(2)
+        read(1, 0, R)
+        weave(slice(0, 2), slice(0, P), slice(0, PACK))
+        spell(3)
+        read(2, 0, R)
+
+        xg_w = keep.tile([P, J], U32, align_bytes=64)
+        xg_s = keep.tile([P, J], U8, align_bytes=64)
+        nc.vector.tensor_copy(xg_w[:], xt_w[:].indirect(list1[:]))
+        nc.vector.tensor_copy(xg_s[:], xt_s[:].indirect(list1[:]))
+
+        read(3, 0, R // 2)
+        weave(slice(2, 4), slice(0, P // 2), slice(0, PACK))
+        read(3, R // 2, R // 2)
+        weave(slice(2, 4), slice(P // 2, P), slice(0, 1))
+        weave(slice(2, 4), slice(P // 2, P), slice(1, PACK))
+
+        a_sb = [keep.tile([P, J], F32, name=f"a{t}") for t in range(PACK)]
+
+        def quantize_wc(t):
+            cols = slice(t * P, (t + 1) * P)
+            nc.vector.quantize_mx(
+                out=wc_w[:, cols].bitcast(FP8X4), scales=wc_s[:, cols],
+                in_=wc_in[:, t].rearrange("p m j -> p (m j)"),
+            )
+
+        def first_product(t, first, count, name):
+            cols = slice(t * P, (t + 1) * P)
+            slots = slice(first, first + count)
+            bank = psum.tile([P, count], F32, name=name)
+            nc.tensor.matmul_mx(
+                out=bank[:], lhsT=wc_w[:, cols].bitcast(FP8X4), lhsT_scale=wc_s[:, cols],
+                rhs=xg_w[:, slots].bitcast(FP8X4), rhs_scale=xg_s[:, slots], start=True, stop=True,
+            )
+            return bank
+
+        for t in range(PACK):
+            quantize_wc(t)
+        for h in range(2):
+            bank = first_product(0, h * J // 2, J // 2, f"a0_bank{h}")
+            nc.scalar.copy(a_sb[0][:, h * J // 2 : (h + 1) * J // 2], bank[:])
+        for t in range(1, PACK):
+            bank = first_product(t, 0, J, f"a{t}_bank")
+            nc.vector.tensor_copy(a_sb[t][:], bank[:])
+
+        one = keep.tile([P, PACK, O], F32)
+        own = keep.tile([P, PACK, O], F32)
+        hid = keep.tile([P, O, PACK], BF16, align_bytes=64)
+        hid_w = keep.tile([P, O], U32, align_bytes=64)
+        hid_s = keep.tile([P, O], U8, align_bytes=64)
+
+        def take(t, first, count):
+            places = slice(first, first + count)
+            fetch(one[:, t, places], a_sb[t], entries(list4, first, count), sa_sb[:, t : t + 1])
+            fetch(own[:, t, places], a_sb[t], entries(list5, first, count), sb_sb[:, t : t + 1])
+
+        def larger(ts, places):
+            nc.vector.tensor_tensor(
+                hid[:, places, ts],
+                one[:].rearrange("p t o -> p o t")[:, places, ts],
+                own[:].rearrange("p t o -> p o t")[:, places, ts],
+                MAX,
+            )
+
+        p_sb = [keep.tile([P, O], F32, name=f"p{b}") for b in range(N // P)]
+
+        def second_product(b, places, bank):
+            cols = slice(b * P, (b + 1) * P)
+            nc.tensor.matmul_mx(
+                out=bank, lhsT=wb_w[:, cols].bitcast(FP8X4), lhsT_scale=wb_s[:, cols],
+                rhs=hid_w[:, places].bitcast(FP8X4), rhs_scale=hid_s[:, places], start=True, stop=True,
+            )
+
+        def quantize_hid(places):
+            nc.vector.quantize_mx(
+                out=hid_w[:, places].bitcast(FP8X4), scales=hid_s[:, places],
+                in_=hid[:, places, :].rearrange("p o t -> p (o t)"),
+            )
+
+        half = O // 2
+        take(0, 0, O)
+        take(1, 0, O)
+        larger(slice(0, 2), slice(0, O))
+        early, late = slice(0, half), slice(half, O)
+        take(2, 0, half)
+        take(3, 0, half)
+        larger(slice(2, 4), early)
+        quantize_hid(early)
+        early_bank = psum.tile([P, N // P, half], F32)
+        for b in range(N // P):
+            second_product(b, early, early_bank[:, b, :])
+        for b in range(N // P):
+            nc.vector.tensor_copy(p_sb[b][:, early], early_bank[:, b, :])
+        take(2, half, half)
+        take(3, half, half)
+        larger(slice(2, 4), late)
+        quantize_hid(late)
+        late_banks = [psum.tile([P, half], F32, name=f"late_bank{b}") for b in range(N // P)]
+        for b in range(N // P):
+            second_product(b, late, late_banks[b][:])
+        nc.scalar.copy(p_sb[0][:, late], late_banks[0][:])
+        nc.vector.tensor_copy(p_sb[1][:, late], late_banks[1][:])
+
+        for b in range(N // P):
+            m0 = keep.tile([P, U], F32, name=f"m0_{b}")
+            fetch(m0[:], p_sb[b], list6[:], so_sb[:, b : b + 1])
+            nc.vector.tensor_copy(pages[b][:].indirect(list7[:]), m0[:])
+            nc.sync.dma_start(out[b * P : (b + 1) * P, :], pages[b][:])

@@ -65,16 +65,29 @@ def tile_picked_tokens_respelled_one_mixedpair_one_posted_kernel(
         ua_planes = ua.rearrange("(p j) f -> j p f", j=PACK)
         ua_sb = [keep.tile([P, F], F32, name=f"ua{j}") for j in range(PACK)]
         ha_sb = load_rows(nc.scalar, ha, "ha_sb")
-        hb_sb = load_rows(nc.scalar, hb, "hb_sb")
+        hb_rows = hb.rearrange("(p j) o -> p (j o)", j=PACK)
+
+        def load_hb(queue, first, count):
+            tile = keep.tile([P, count], F32, name=f"hb{first}")
+            with nc.allow_non_contiguous_dma(reason="one or two weights a partition"):
+                queue.dma_start(tile[:], hb_rows[:, first : first + count])
+            return [tile[:, i : i + 1] for i in range(count)]
+
+        xt_w = keep.tile([P, T], U32, align_bytes=64)
+        xt_rows = xt_words[0].rearrange("p n t -> p (n t)").bitcast(I32)
+        hb_cols = load_hb(nc.scalar, 0, 1)
         nc.sync.dma_start(ua_sb[0][:], ua_planes[0])
         list2 = load_list(offs2, "list2")
         nc.sync.dma_start(ua_sb[1][:], ua_planes[1])
         list3 = load_list(offs3, "list3")
-        nc.sync.dma_start(ua_sb[2][:], ua_planes[2])
-        nc.sync.dma_start(ua_sb[3][:], ua_planes[3])
         list1 = load_list(offs, "list1")
-        xt_w = load_words(xt_words, "xt_w")
         load_scales(xt_s, xt_scales)
+        nc.sync.dma_start(ua_sb[2][:], ua_planes[2])
+        hb_cols.extend(load_hb(nc.sync, 1, 1))
+        nc.sync.dma_start(xt_w[:, : T // 2].bitcast(I32), xt_rows[:, : T // 2])
+        nc.sync.dma_start(ua_sb[3][:], ua_planes[3])
+        hb_cols.extend(load_hb(nc.sync, 2, 2))
+        nc.sync.dma_start(xt_w[:, T // 2 :].bitcast(I32), xt_rows[:, T // 2 :])
         list4 = load_list(offs4, "list4")
         list5 = load_list(offs5, "list5")
         sa_sb = load_rows(nc.sync, sa, "sa_sb")
@@ -97,7 +110,7 @@ def tile_picked_tokens_respelled_one_mixedpair_one_posted_kernel(
             fetch(wcd[j][:], ua_sb[j], list2[:], ha_sb[:, j : j + 1])
 
         def read(j, first, count):
-            fetch(wc[:, j, first : first + count], wcd[j], entries(list3, first, count), hb_sb[:, j : j + 1])
+            fetch(wc[:, j, first : first + count], wcd[j], entries(list3, first, count), hb_cols[j])
 
         def weave(js, ms, ts):
             nc.vector.tensor_copy(
@@ -116,23 +129,28 @@ def tile_picked_tokens_respelled_one_mixedpair_one_posted_kernel(
 
         xg_w = keep.tile([P, J], U32, align_bytes=64)
         xg_s = keep.tile([P, J], U8, align_bytes=64)
-        nc.vector.tensor_copy(xg_w[:], xt_w[:].indirect(list1[:]))
         nc.vector.tensor_copy(xg_s[:], xt_s[:].indirect(list1[:]))
+        nc.vector.tensor_copy(xg_w[:], xt_w[:].indirect(list1[:]))
 
-        read(3, 0, R // 2)
-        weave(slice(2, 4), slice(0, P // 2), slice(0, PACK))
-        read(3, R // 2, R // 2)
-        weave(slice(2, 4), slice(P // 2, P), slice(0, 1))
-        weave(slice(2, 4), slice(P // 2, P), slice(1, PACK))
-
-        a_sb = [keep.tile([P, J], F32, name=f"a{t}") for t in range(PACK)]
-
-        def quantize_wc(t):
-            cols = slice(t * P, (t + 1) * P)
+        def quantize_wc(t, ms):
+            cols = slice(t * P + ms.start, t * P + ms.stop)
             nc.vector.quantize_mx(
                 out=wc_w[:, cols].bitcast(FP8X4), scales=wc_s[:, cols],
-                in_=wc_in[:, t].rearrange("p m j -> p (m j)"),
+                in_=wc_in[:, t, ms, :].rearrange("p m j -> p (m j)"),
             )
+
+        low, high = slice(0, P // 2), slice(P // 2, P)
+        read(3, 0, R // 2)
+        weave(slice(2, 4), low, slice(0, PACK))
+        read(3, R // 2, R // 2)
+        weave(slice(2, 4), high, slice(0, 1))
+        weave(slice(2, 4), high, slice(1, 2))
+        quantize_wc(0, slice(0, P))
+        weave(slice(2, 4), high, slice(2, PACK))
+        for t in range(1, PACK):
+            quantize_wc(t, slice(0, P))
+
+        a_sb = [keep.tile([P, J], F32, name=f"a{t}") for t in range(PACK)]
 
         def first_product(t, first, count, name):
             cols = slice(t * P, (t + 1) * P)
@@ -144,8 +162,6 @@ def tile_picked_tokens_respelled_one_mixedpair_one_posted_kernel(
             )
             return bank
 
-        for t in range(PACK):
-            quantize_wc(t)
         for h in range(2):
             bank = first_product(0, h * J // 2, J // 2, f"a0_bank{h}")
             nc.scalar.copy(a_sb[0][:, h * J // 2 : (h + 1) * J // 2], bank[:])
@@ -192,17 +208,16 @@ def tile_picked_tokens_respelled_one_mixedpair_one_posted_kernel(
         take(1, 0, O)
         larger(slice(0, 2), slice(0, O))
         early, late = slice(0, half), slice(half, O)
-        take(2, 0, half)
+        take(2, 0, O)
         take(3, 0, half)
         larger(slice(2, 4), early)
         quantize_hid(early)
         early_bank = psum.tile([P, N // P, half], F32)
         for b in range(N // P):
             second_product(b, early, early_bank[:, b, :])
-        for b in range(N // P):
-            nc.vector.tensor_copy(p_sb[b][:, early], early_bank[:, b, :])
-        take(2, half, half)
         take(3, half, half)
+        for b in range(N // P):
+            nc.scalar.copy(p_sb[b][:, early], early_bank[:, b, :])
         larger(slice(2, 4), late)
         quantize_hid(late)
         late_banks = [psum.tile([P, half], F32, name=f"late_bank{b}") for b in range(N // P)]

@@ -100,6 +100,11 @@ def tile_picked_tokens_respelled_one_mixedpair_one_posted_kernel(
         with nc.allow_non_contiguous_dma(reason="one weight a partition for each block of output features"):
             nc.sync.dma_start(so_sb[:], so.rearrange("(b p) o -> p (b o)", p=P))
 
+        warm_in = keep.tile([P, 1], F32)
+        warm_out = keep.tile([P, 1], F32)
+        nc.vector.memset(warm_in[:], 0.0)
+        nc.scalar.activation(warm_out[:], warm_in[:], COPY)
+
         wcd = [keep.tile([P, G], F32, name=f"wcd{j}") for j in range(PACK)]
         wc = keep.tile([P, PACK, R], BF16)
         wc_in = keep.tile([P, PACK, P, PACK], BF16, align_bytes=64)

from contextlib import ExitStack

import concourse.mybir as mybir

K, J, R, T, F, G, O, N, U, E = 512, 512, 512, 2048, 2048, 1024, 256, 256, 128, 512
FLOPS = 2 * K * R * J + 2 * R * N * O

F32 = mybir.dt.float32
BF16 = mybir.dt.bfloat16
I32 = mybir.dt.int32
U32 = mybir.dt.uint32
U16 = mybir.dt.uint16
U8 = mybir.dt.uint8
FP8X4 = mybir.dt.float8_e4m3fn_x4
COPY = mybir.ActivationFunctionType.Copy
MAX = mybir.AluOpType.max

P = 128
PACK = 4
LANES = 16


def tile_picked_tokens_respelled_one_mixedpair_one_posted_kernel(
    tc, xt_words, xt_scales, ua, ha, hb, sa, sb, wb_words, wb_scales, so,
    offs, offs2, offs3, offs4, offs5, offs6, offs7, out,
):
    nc = tc.nc
    with ExitStack() as ctx:
        keep = ctx.enter_context(tc.tile_pool(name="keep", bufs=1))
        psum = ctx.enter_context(tc.psum_pool(name="psum", bufs=1))

        def load_list(src, name):
            tile = keep.tile(list(src.shape), U16, name=name)
            nc.sync.dma_start(tile[:], src)
            return tile

        def load_rows(queue, src, name):
            tile = keep.tile([P, PACK], F32, name=name)
            queue.dma_start(tile[:], src.rearrange("(p j) o -> p (j o)", j=PACK))
            return tile

        def load_words(src, name):
            tile = keep.tile([P, src.shape[2]], U32, name=name, align_bytes=64)
            nc.sync.dma_start(tile[:].bitcast(I32), src[0].rearrange("p n t -> p (n t)").bitcast(I32))
            return tile

        def load_scales(tile, src):
            for q in range(4):
                nc.sync.dma_start(tile[32 * q : 32 * q + 4, :].bitcast(I32), src[0, 4 * q : 4 * q + 4, :].bitcast(I32))

        def entries(lists, first, count):
            return lists[:, first // LANES : (first + count) // LANES]

        def fetch(dst, window, offsets, scale):
            nc.scalar.activation(dst, window[:].indirect(offsets), COPY, scale=scale)

        xt_s = keep.tile([P, T], U8, align_bytes=64)
        wb_s = keep.tile([P, N], U8, align_bytes=64)
        pages = [keep.tile([P, E], F32, name=f"page{b}") for b in range(N // P)]
        nc.vector.memset(xt_s[:].bitcast(I32), 0)
        nc.vector.memset(wb_s[:].bitcast(I32), 0)
        for page in pages:
            nc.vector.memset(page[:], 0.0)

        ua_planes = ua.rearrange("(p j) f -> j p f", j=PACK)
        ua_sb = [keep.tile([P, F], F32, name=f"ua{j}") for j in range(PACK)]
        ha_sb = load_rows(nc.scalar, ha, "ha_sb")
        hb_rows = hb.rearrange("(p j) o -> p (j o)", j=PACK)

        def load_hb(queue, first, count):
            tile = keep.tile([P, count], F32, name=f"hb{first}")
            with nc.allow_non_contiguous_dma(reason="one or two weights a partition"):
                queue.dma_start(tile[:], hb_rows[:, first : first + count])
            return [tile[:, i : i + 1] for i in range(count)]

        xt_w = keep.tile([P, T], U32, align_bytes=64)
        xt_rows = xt_words[0].rearrange("p n t -> p (n t)").bitcast(I32)
        hb_cols = load_hb(nc.scalar, 0, 1)
        nc.sync.dma_start(ua_sb[0][:], ua_planes[0])
        list2 = load_list(offs2, "list2")
        nc.sync.dma_start(ua_sb[1][:], ua_planes[1])
        list3 = load_list(offs3, "list3")
        list1 = load_list(offs, "list1")
        load_scales(xt_s, xt_scales)
        nc.sync.dma_start(ua_sb[2][:], ua_planes[2])
        hb_cols.extend(load_hb(nc.sync, 1, 1))
        nc.sync.dma_start(xt_w[:, : T // 2].bitcast(I32), xt_rows[:, : T // 2])
        nc.sync.dma_start(ua_sb[3][:], ua_planes[3])
        hb_cols.extend(load_hb(nc.sync, 2, 2))
        nc.sync.dma_start(xt_w[:, T // 2 :].bitcast(I32), xt_rows[:, T // 2 :])
        list4 = load_list(offs4, "list4")
        list5 = load_list(offs5, "list5")
        sa_sb = load_rows(nc.sync, sa, "sa_sb")
        sb_sb = load_rows(nc.sync, sb, "sb_sb")
        wb_w = load_words(wb_words, "wb_w")
        load_scales(wb_s, wb_scales)
        list6 = load_list(offs6, "list6")
        list7 = load_list(offs7, "list7")
        so_sb = keep.tile([P, N // P], F32)
        with nc.allow_non_contiguous_dma(reason="one weight a partition for each block of output features"):
            nc.sync.dma_start(so_sb[:], so.rearrange("(b p) o -> p (b o)", p=P))

        warm_in = keep.tile([P, 1], F32)
        warm_out = keep.tile([P, 1], F32)
        nc.vector.memset(warm_in[:], 0.0)
        nc.scalar.activation(warm_out[:], warm_in[:], COPY)

        wcd = [keep.tile([P, G], F32, name=f"wcd{j}") for j in range(PACK)]
        wc = keep.tile([P, PACK, R], BF16)
        wc_in = keep.tile([P, PACK, P, PACK], BF16, align_bytes=64)
        wc_w = keep.tile([P, R], U32, align_bytes=64)
        wc_s = keep.tile([P, R], U8, align_bytes=64)

        def spell(j):
            fetch(wcd[j][:], ua_sb[j], list2[:], ha_sb[:, j : j + 1])

        def read(j, first, count):
            fetch(wc[:, j, first : first + count], wcd[j], entries(list3, first, count), hb_cols[j])

        def weave(js, ms, ts):
            nc.vector.tensor_copy(
                out=wc_in[:].rearrange("p t m j -> p m t j")[:, ms, ts, js],
                in_=wc[:].rearrange("p j (m t) -> p m t j", t=PACK)[:, ms, ts, js],
            )

        spell(0)
        spell(1)
        read(0, 0, R)
        spell(2)
        read(1, 0, R)
        weave(slice(0, 2), slice(0, P), slice(0, PACK))
        spell(3)
        read(2, 0, R)

        xg_w = keep.tile([P, J], U32, align_bytes=64)
        xg_s = keep.tile([P, J], U8, align_bytes=64)
        nc.vector.tensor_copy(xg_s[:], xt_s[:].indirect(list1[:]))
        nc.vector.tensor_copy(xg_w[:], xt_w[:].indirect(list1[:]))

        def quantize_wc(t, ms):
            cols = slice(t * P + ms.start, t * P + ms.stop)
            nc.vector.quantize_mx(
                out=wc_w[:, cols].bitcast(FP8X4), scales=wc_s[:, cols],
                in_=wc_in[:, t, ms, :].rearrange("p m j -> p (m j)"),
            )

        low, high = slice(0, P // 2), slice(P // 2, P)
        read(3, 0, R // 2)
        weave(slice(2, 4), low, slice(0, PACK))
        read(3, R // 2, R // 2)
        weave(slice(2, 4), high, slice(0, 1))
        weave(slice(2, 4), high, slice(1, 2))
        quantize_wc(0, slice(0, P))
        weave(slice(2, 4), high, slice(2, PACK))
        for t in range(1, PACK):
            quantize_wc(t, slice(0, P))

        a_sb = [keep.tile([P, J], F32, name=f"a{t}") for t in range(PACK)]

        def first_product(t, first, count, name):
            cols = slice(t * P, (t + 1) * P)
            slots = slice(first, first + count)
            bank = psum.tile([P, count], F32, name=name)
            nc.tensor.matmul_mx(
                out=bank[:], lhsT=wc_w[:, cols].bitcast(FP8X4), lhsT_scale=wc_s[:, cols],
                rhs=xg_w[:, slots].bitcast(FP8X4), rhs_scale=xg_s[:, slots], start=True, stop=True,
            )
            return bank

        for h in range(2):
            bank = first_product(0, h * J // 2, J // 2, f"a0_bank{h}")
            nc.scalar.copy(a_sb[0][:, h * J // 2 : (h + 1) * J // 2], bank[:])
        for t in range(1, PACK):
            bank = first_product(t, 0, J, f"a{t}_bank")
            nc.vector.tensor_copy(a_sb[t][:], bank[:])

        one = keep.tile([P, PACK, O], F32)
        own = keep.tile([P, PACK, O], F32)
        hid = keep.tile([P, O, PACK], BF16, align_bytes=64)
        hid_w = keep.tile([P, O], U32, align_bytes=64)
        hid_s = keep.tile([P, O], U8, align_bytes=64)

        def take(t, first, count):
            places = slice(first, first + count)
            fetch(one[:, t, places], a_sb[t], entries(list4, first, count), sa_sb[:, t : t + 1])
            fetch(own[:, t, places], a_sb[t], entries(list5, first, count), sb_sb[:, t : t + 1])

        def larger(ts, places):
            nc.vector.tensor_tensor(
                hid[:, places, ts],
                one[:].rearrange("p t o -> p o t")[:, places, ts],
                own[:].rearrange("p t o -> p o t")[:, places, ts],
                MAX,
            )

        p_sb = [keep.tile([P, O], F32, name=f"p{b}") for b in range(N // P)]

        def second_product(b, places, bank):
            cols = slice(b * P, (b + 1) * P)
            nc.tensor.matmul_mx(
                out=bank, lhsT=wb_w[:, cols].bitcast(FP8X4), lhsT_scale=wb_s[:, cols],
                rhs=hid_w[:, places].bitcast(FP8X4), rhs_scale=hid_s[:, places], start=True, stop=True,
            )

        def quantize_hid(places):
            nc.vector.quantize_mx(
                out=hid_w[:, places].bitcast(FP8X4), scales=hid_s[:, places],
                in_=hid[:, places, :].rearrange("p o t -> p (o t)"),
            )

        half = O // 2
        take(0, 0, O)
        take(1, 0, O)
        larger(slice(0, 2), slice(0, O))
        early, late = slice(0, half), slice(half, O)
        take(2, 0, O)
        take(3, 0, half)
        larger(slice(2, 4), early)
        quantize_hid(early)
        early_bank = psum.tile([P, N // P, half], F32)
        for b in range(N // P):
            second_product(b, early, early_bank[:, b, :])
        take(3, half, half)
        for b in range(N // P):
            nc.scalar.copy(p_sb[b][:, early], early_bank[:, b, :])
        larger(slice(2, 4), late)
        quantize_hid(late)
        late_banks = [psum.tile([P, half], F32, name=f"late_bank{b}") for b in range(N // P)]
        for b in range(N // P):
            second_product(b, late, late_banks[b][:])
        nc.scalar.copy(p_sb[0][:, late], late_banks[0][:])
        nc.vector.tensor_copy(p_sb[1][:, late], late_banks[1][:])

        for b in range(N // P):
            m0 = keep.tile([P, U], F32, name=f"m0_{b}")
            fetch(m0[:], p_sb[b], list6[:], so_sb[:, b : b + 1])
            nc.vector.tensor_copy(pages[b][:].indirect(list7[:]), m0[:])
            nc.sync.dma_start(out[b * P : (b + 1) * P, :], pages[b][:])
